import numpy as np
import ml_dtypes


def mxq(x, axis, fmt="e4m3"):
    dtype, down = {"e4m3": (ml_dtypes.float8_e4m3fn, 7), "e5m2": (ml_dtypes.float8_e5m2, 14)}[fmt]
    v = np.moveaxis(np.asarray(x, np.float32).astype(ml_dtypes.bfloat16).astype(np.float64), axis, -1)
    blocks = v.reshape(v.shape[:-1] + (-1, 32))
    amax = np.abs(blocks).max(-1, keepdims=True)
    byte = np.maximum(np.where(amax > 0, np.frexp(amax)[1] - 1 + 127, 0) - down, 1)
    scale = np.exp2(byte - 127.0)
    codes = (blocks / scale).astype(np.float32).astype(dtype).astype(np.float64)
    return np.moveaxis((codes * scale).reshape(v.shape), -1, axis)


WIDE = False


def mx_kscale(k):
    if not WIDE:
        return np.ones(k)
    levels = np.array([30, -30])
    if k % 512:
        return np.exp2(np.random.permutation(np.resize(levels, k // 32))).repeat(32)
    a = np.empty((k // 512, 16))
    for p in range(k // 512):
        a[p, :8] = np.random.permutation(np.resize(levels, 8))
        for g in range(8):
            far = levels[np.abs(levels - a[p, g]) >= 10]
            a[p, g + 8] = far[np.random.randint(len(far))]
    return np.exp2(a.ravel()).repeat(32)


def f64(x):
    return np.asarray(x).astype(np.float64)


def striped(idx):
    return np.tile(np.asarray(idx).reshape(-1, 16).T, (8, 1)).astype(np.uint16)


def unstriped(offs):
    return offs[:16].T.reshape(-1).astype(np.int64)


E2M1 = np.array([0.0, 0.5, 1.0, 1.5, 2.0, 3.0, 4.0, 6.0, -0.0, -0.5, -1.0, -1.5, -2.0, -3.0, -4.0, -6.0])


def pack_weight(w, fmt):
    k, n = w.shape
    w = f64(np.asarray(w, np.float32).astype(ml_dtypes.bfloat16)).reshape(k // 32, 32, n)
    amax = np.abs(w).max(1)
    if fmt in ("e4m3", "e5m2"):
        byte = np.frexp(amax)[1] - 1 + 127 - (7 if fmt == "e4m3" else 14)
    else:
        mant, ex = np.frexp(amax / 6.0)
        byte = np.where(mant > 0.5, ex, ex - 1) + 127
    byte = np.clip(np.where(amax > 0, byte, 1), 1, 254)
    scaled = (w * np.exp2(127.0 - byte)[:, None, :]).reshape(k, n).astype(np.float32)
    by_word = np.ascontiguousarray(scaled.reshape(k // 512, 128, 4, n).transpose(0, 1, 3, 2))
    if fmt in ("e4m3", "e5m2"):
        words = by_word.astype(ml_dtypes.float8_e4m3fn if fmt == "e4m3" else ml_dtypes.float8_e5m2).view(np.uint8)
    else:
        c = by_word.astype(ml_dtypes.float4_e2m1fn).view(np.uint8) & 0xF
        words = (c[..., 0::2] | (c[..., 1::2] << 4)).reshape(k // 512, 128, 2 * n)
    return np.ascontiguousarray(words), np.ascontiguousarray(byte.astype(np.uint8).reshape(k // 512, 16, n))


def unpack_weight(words, scales, fmt):
    g, _, n = scales.shape
    words = np.ascontiguousarray(words).reshape(g, 128, n, -1)
    if fmt in ("e4m3", "e5m2"):
        vals = words.view(ml_dtypes.float8_e4m3fn if fmt == "e4m3" else ml_dtypes.float8_e5m2).astype(np.float64)
    else:
        nib = np.empty((g, 128, n, 4), np.uint8)
        nib[..., 0::2] = words & 0xF
        nib[..., 1::2] = words >> 4
        vals = E2M1[nib]
    vals = vals * np.repeat(np.exp2(scales.astype(np.float64) - 127.0), 8, axis=1)[..., None]
    return vals.transpose(0, 1, 3, 2).reshape(g * 512, n)


K, T, J, R, V, N, Z = 1024, 1024, 256, 512, 512, 256, 512


def setup_inputs():
    n = np.random.standard_normal
    idx = np.random.permutation(T)[:J]
    idx2 = np.random.permutation(V)[:J]
    idx3 = np.random.permutation(V)[:J]
    idx4 = np.random.permutation(Z)[:J]
    fk = mx_kscale(K)
    fr = mx_kscale(R)
    wp = pack_weight(n((K, R)) * 1 / np.sqrt(K) * fk[:, None] * fr, "e5m2")
    return {
        "xf": (n((K, T))).astype(np.float32),
        "fk": (np.random.uniform(0.5, 2.0, (K, 1)) / fk[:, None]).astype(np.float32),
        "w_words": wp[0],
        "w_scales": wp[1],
        "tb": (n((R, V)) * 0.7 * fr[:, None]).astype(np.float32),
        "wb": (n((R, N)) * 1 / np.sqrt(R) / fr[:, None]).astype(np.float32),
        "tz": (n((N, Z))).astype(np.float32),
        "offs": striped(idx),
        "offs2": striped(idx2),
        "offs3": striped(idx3),
        "offs4": striped(idx4),
    }


def reference(xf, fk, w_words, w_scales, tb, wb, tz, offs, offs2, offs3, offs4):
    idx = unstriped(offs)
    idx2 = unstriped(offs2)
    idx3 = unstriped(offs3)
    idx4 = unstriped(offs4)
    wu = unpack_weight(w_words, w_scales, "e5m2")
    xg = f64(xf)[:, idx]
    x1 = np.pad(xg, ((0, 0), (1, 0)))[:, :J]
    u = (xg - 0.6 * x1) * f64(fk)
    uq = mxq(u, 0, "e4m3")
    a = wu.T @ uq
    hid = np.maximum(a + f64(tb)[:, idx2] - f64(tb)[:, idx3], 0.0)
    wbq = mxq(f64(wb), 0, "e5m2")
    hidq = mxq(hid, 0, "e5m2")
    p = wbq.T @ hidq
    y = p * f64(tz)[:, idx4]
    return y

@@ -1,0 +1,193 @@
+from contextlib import ExitStack
+
+import concourse.mybir as mybir
+
+K, T, J, R, V, N, Z = 1024, 1024, 256, 512, 512, 256, 512
+FLOPS = 2 * K * R * J + 2 * R * N * J
+
+F32 = mybir.dt.float32
+BF16 = mybir.dt.bfloat16
+I32 = mybir.dt.int32
+U32 = mybir.dt.uint32
+U16 = mybir.dt.uint16
+U8 = mybir.dt.uint8
+E4M3 = mybir.dt.float8_e4m3fn_x4
+E5M2 = mybir.dt.float8_e5m2_x4
+ALU = mybir.AluOpType
+ACT = mybir.ActivationFunctionType
+
+P = 128
+PACK = 4
+PASSES = K // (P * PACK)
+HALF = J // 2
+LEAD = 8
+
+
+def weave_out(tile_ap):
+    return tile_ap.rearrange("p (c i t) -> p c t i", i=4, t=PACK)
+
+
+def weave_in(planes_ap):
+    return planes_ap.rearrange("p t (c i) -> p c t i", i=4)
+
+
+def tile_list_steps_tworeach_timeslook_kernel(tc, xf, fk, w_words, w_scales, tb, wb, tz, offs, offs2, offs3, offs4, out):
+    nc = tc.nc
+    with ExitStack() as ctx:
+        keep = ctx.enter_context(tc.tile_pool(name="keep", bufs=1))
+        psum = ctx.enter_context(tc.psum_pool(name="psum", bufs=1))
+
+        l1 = keep.tile([P, J // 16], U16, name="l1")
+        l2 = keep.tile([P, J // 16], U16, name="l2")
+        l3 = keep.tile([P, J // 16], U16, name="l3")
+        l4 = keep.tile([P, J // 16], U16, name="l4")
+        x_pl = [[keep.tile([P, T], F32, name=f"x{a}{t}") for t in range(PACK)] for a in range(PASSES)]
+        tb_pl = [keep.tile([P, V], F32, name=f"tb{t}") for t in range(PACK)]
+        w_raw = [keep.tile([P, R], U32, name=f"wraw{a}") for a in range(PASSES)]
+        ws_raw = keep.tile([P, PASSES, R], U8, name="wsraw")
+        fk_sb = keep.tile([P, PASSES, PACK], F32, name="fk")
+        wb_raw = keep.tile([P, PACK, N], F32, name="wbraw")
+        tz_sb = [keep.tile([P, Z], F32, name=f"tz{h}") for h in range(2)]
+
+        xv = xf.rearrange("(a p t) c -> a t p c", a=PASSES, t=PACK)
+        tbv = tb.rearrange("(p t) v -> t p v", t=PACK)
+
+        def load_w(a):
+            nc.sync.dma_start(out=w_raw[a][:].bitcast(I32), in_=w_words[a].rearrange("p n t -> p (n t)").bitcast(I32))
+
+        def load_scales(q):
+            nc.sync.dma_start(
+                out=ws_raw[32 * q : 32 * q + 4, :, :].bitcast(I32),
+                in_=w_scales[:, 4 * q : 4 * q + 4, :].rearrange("a r n -> r a n").bitcast(I32),
+            )
+
+        def load_x(a, t):
+            nc.sync.dma_start(out=x_pl[a][t][:], in_=xv[a, t])
+
+        nc.vector.memset(ws_raw[:].rearrange("p a n -> p (a n)").bitcast(I32), 0)
+
+        nc.sync.dma_start(out=tb_pl[0][:], in_=tbv[0])
+        nc.sync.dma_start(l3[:], offs3)
+        nc.sync.dma_start(out=tb_pl[1][:], in_=tbv[1])
+        nc.sync.dma_start(l2[:], offs2)
+        nc.sync.dma_start(out=tb_pl[2][:], in_=tbv[2])
+        nc.sync.dma_start(l1[:], offs)
+        load_x(0, 0)
+        nc.sync.dma_start(out=fk_sb[:], in_=fk.rearrange("(a p t) o -> p a (t o)", a=PASSES, t=PACK))
+        load_x(0, 1)
+        load_scales(0)
+        load_w(0)
+        load_scales(1)
+        load_x(0, 2)
+        load_scales(2)
+        load_x(0, 3)
+        load_scales(3)
+        load_w(1)
+        for t in range(PACK):
+            load_x(1, t)
+        nc.sync.dma_start(out=tb_pl[3][:], in_=tbv[3])
+        nc.sync.dma_start(out=wb_raw[:], in_=wb.rearrange("(p t) n -> p t n", t=PACK))
+        nc.sync.dma_start(l4[:], offs4)
+        for h in range(2):
+            nc.sync.dma_start(out=tz_sb[h][:], in_=tz[h * P : (h + 1) * P, :])
+
+        d = keep.tile([P, PACK, J], F32, name="d")
+        t3 = keep.tile([P, PACK, J], F32, name="t3")
+        t2 = keep.tile([P, J], F32, name="t2")
+
+        def table_difference(t):
+            nc.scalar.activation(t3[:, t, :], tb_pl[t][:].indirect(l3[:]), ACT.Copy)
+            if t < PACK - 1:
+                nc.vector.tensor_tensor(d[:, t, :], tb_pl[t][:].indirect(l2[:]), t3[:, t, :], ALU.subtract)
+            else:
+                nc.scalar.activation(t2[:], tb_pl[t][:].indirect(l2[:]), ACT.Copy)
+                nc.vector.tensor_tensor(d[:, t, :], t2[:], t3[:, t, :], ALU.subtract)
+
+        for t in range(PACK - 1):
+            table_difference(t)
+
+        w_c = [keep.tile([P, R], U32, name=f"wc{a}", align_bytes=64) for a in range(PASSES)]
+        w_s = keep.tile([P, PASSES, R], U8, name="ws", align_bytes=64)
+        for a in range(PASSES):
+            nc.vector.tensor_copy(
+                out=w_c[a][:].rearrange("p (t c i) -> p c t i", t=PACK, i=4),
+                in_=w_raw[a][:].rearrange("p (c i t) -> p c t i", t=PACK, i=4),
+            )
+        for a in range(PASSES):
+            nc.vector.tensor_copy(
+                out=w_s[:, a, :].rearrange("p (t m) -> p t m", t=PACK),
+                in_=ws_raw[:, a, :].rearrange("p (m t) -> p t m", t=PACK),
+            )
+
+        acc = [psum.tile([P, PACK, HALF], F32, name=f"acc{b}") for b in range(2)]
+        for a in range(PASSES):
+            g = keep.tile([P, PACK, LEAD + J], F32, name=f"g{a}")
+            nc.vector.memset(g[:, :, 0:LEAD], 0.0)
+            e = keep.tile([P, PACK, J], F32, name=f"e{a}")
+            ub = keep.tile([P, PACK, J], BF16, name=f"ub{a}")
+            uw = keep.tile([P, J * PACK], BF16, name=f"uw{a}", align_bytes=64)
+            u_c = keep.tile([P, J], U32, name=f"uc{a}", align_bytes=64)
+            u_s = keep.tile([P, J], U8, name=f"us{a}", align_bytes=64)
+            for t in range(PACK):
+                nc.scalar.activation(g[:, t, LEAD:], x_pl[a][t][:].indirect(l1[:]), ACT.Copy)
+                nc.vector.scalar_tensor_tensor(
+                    out=e[:, t, :], in0=g[:, t, LEAD - 1 : LEAD - 1 + J], scalar=-0.6, in1=g[:, t, LEAD:], op0=ALU.mult, op1=ALU.add
+                )
+                nc.vector.tensor_scalar_mul(ub[:, t, :], e[:, t, :], fk_sb[:, a, t : t + 1])
+            for b in range(2):
+                js = slice(b * HALF, (b + 1) * HALF)
+                nc.vector.tensor_copy(out=weave_out(uw[:, b * HALF * PACK : (b + 1) * HALF * PACK]), in_=weave_in(ub[:, :, js]))
+            for b in range(2):
+                js = slice(b * HALF, (b + 1) * HALF)
+                nc.vector.quantize_mx(out=u_c[:, js].bitcast(E4M3), scales=u_s[:, js], in_=uw[:, b * HALF * PACK : (b + 1) * HALF * PACK])
+                for t in range(PACK):
+                    ms = slice(t * P, (t + 1) * P)
+                    nc.tensor.matmul_mx(
+                        out=acc[b][:, t, :],
+                        lhsT=w_c[a][:, ms].bitcast(E5M2),
+                        lhsT_scale=w_s[:, a, ms],
+                        rhs=u_c[:, js].bitcast(E4M3),
+                        rhs_scale=u_s[:, js],
+                        start=(a == 0 and t == 0),
+                        stop=(a == PASSES - 1 and t == PACK - 1),
+                    )
+
+        table_difference(PACK - 1)
+
+        wbw = keep.tile([P, N * PACK], BF16, name="wbw", align_bytes=64)
+        wb_c = keep.tile([P, N], U32, name="wbc", align_bytes=64)
+        wb_s = keep.tile([P, N], U8, name="wbs", align_bytes=64)
+        nc.scalar.copy(out=weave_out(wbw[:]), in_=weave_in(wb_raw[:]))
+        nc.vector.quantize_mx(out=wb_c[:].bitcast(E5M2), scales=wb_s[:], in_=wbw[:])
+
+        s = [keep.tile([P, PACK, HALF], F32, name=f"s{b}") for b in range(2)]
+        hw = [keep.tile([P, HALF * PACK], BF16, name=f"hw{b}", align_bytes=64) for b in range(2)]
+        h_c = [keep.tile([P, HALF], U32, name=f"hc{b}", align_bytes=64) for b in range(2)]
+        h_s = [keep.tile([P, HALF], U8, name=f"hs{b}", align_bytes=64) for b in range(2)]
+        pr = [psum.tile([P, 2, HALF], F32, name=f"pr{b}") for b in range(2)]
+        res = [keep.tile([P, 2, HALF], F32, name=f"res{b}") for b in range(2)]
+        tzg = keep.tile([P, 2, J], F32, name="tzg")
+        for b in range(2):
+            nc.vector.tensor_tensor(s[b][:], acc[b][:], d[:, :, b * HALF : (b + 1) * HALF], ALU.add)
+        nc.scalar.activation(weave_out(hw[0][:]), weave_in(s[0][:]), ACT.Relu)
+        nc.vector.tensor_scalar_max(weave_out(hw[1][:]), weave_in(s[1][:]), 0.0)
+        for h in range(2):
+            nc.scalar.activation(tzg[:, h, :], tz_sb[h][:].indirect(l4[:]), ACT.Copy)
+        for b in range(2):
+            nc.vector.quantize_mx(out=h_c[b][:].bitcast(E5M2), scales=h_s[b][:], in_=hw[b][:])
+            for h in range(2):
+                ns = slice(h * P, (h + 1) * P)
+                nc.tensor.matmul_mx(
+                    out=pr[b][:, h, :],
+                    lhsT=wb_c[:, ns].bitcast(E5M2),
+                    lhsT_scale=wb_s[:, ns],
+                    rhs=h_c[b][:].bitcast(E5M2),
+                    rhs_scale=h_s[b][:],
+                    start=True,
+                    stop=True,
+                )
+        ov = out.rearrange("(h p) j -> p h j", p=P)
+        for b in range(2):
+            js = slice(b * HALF, (b + 1) * HALF)
+            nc.vector.tensor_tensor(res[b][:], pr[b][:], tzg[:, :, js], ALU.mult)
+            nc.sync.dma_start(out=ov[:, :, js], in_=res[b][:])

@@ -42,50 +42,43 @@ def tile_list_steps_tworeach_timeslook_kernel(tc, xf, fk, w_words, w_scales, tb,
         l3 = keep.tile([P, J // 16], U16, name="l3")
         l4 = keep.tile([P, J // 16], U16, name="l4")
         x_pl = [[keep.tile([P, T], F32, name=f"x{a}{t}") for t in range(PACK)] for a in range(PASSES)]
-        tb_pl = [keep.tile([P, V], F32, name=f"tb{t}") for t in range(PACK)]
+        tb_lo = [keep.tile([P, V], F32, name=f"tb{t}") for t in range(2)]
+        tb_hi = keep.tile([P, 2, V], F32, name="tbhi")
         w_raw = [keep.tile([P, R], U32, name=f"wraw{a}") for a in range(PASSES)]
         ws_raw = keep.tile([P, PASSES, R], U8, name="wsraw")
-        fk_sb = keep.tile([P, PASSES, PACK], F32, name="fk")
+        fk_sb = keep.tile([P, PASSES, 8], F32, name="fk")
         wb_raw = keep.tile([P, PACK, N], F32, name="wbraw")
         tz_sb = [keep.tile([P, Z], F32, name=f"tz{h}") for h in range(2)]
 
         xv = xf.rearrange("(a p t) c -> a t p c", a=PASSES, t=PACK)
-        tbv = tb.rearrange("(p t) v -> t p v", t=PACK)
+        tbv = tb.rearrange("(p t) v -> p t v", t=PACK)
 
-        def load_w(a):
-            nc.sync.dma_start(out=w_raw[a][:].bitcast(I32), in_=w_words[a].rearrange("p n t -> p (n t)").bitcast(I32))
+        wv = w_words.rearrange("a p n t -> a p (n t)").bitcast(I32)
 
-        def load_scales(q):
+        gs = [keep.tile([P, PACK, LEAD + J], F32, name=f"g{a}") for a in range(PASSES)]
+        nc.vector.memset(gs[0][:, :, 0:LEAD], 0.0)
+        nc.scalar.activation(gs[1][:, :, 0:LEAD], gs[0][:, :, 0:LEAD], ACT.Copy)
+        nc.gpsimd.memset(ws_raw[:].rearrange("p a n -> p (a n)").bitcast(I32), 0)
+
+        nc.sync.dma_start(out=tb_lo[0][:], in_=tbv[:, 0, :])
+        nc.sync.dma_start(l3[:], offs3)
+        nc.sync.dma_start(l2[:], offs2)
+        nc.sync.dma_start(out=tb_lo[1][:], in_=tbv[:, 1, :])
+        nc.sync.dma_start(out=tb_hi[:], in_=tbv[:, 2:4, :])
+        nc.sync.dma_start(l1[:], offs)
+        nc.sync.dma_start(out=w_raw[1][:].bitcast(I32), in_=wv[1])
+        nc.sync.dma_start(out=x_pl[0][0][:], in_=xv[0, 0])
+        nc.sync.dma_start(out=fk_sb[:, :, 0:PACK], in_=fk.rearrange("(a p t) o -> p a (t o)", a=PASSES, t=PACK))
+        for q in range(4):
             nc.sync.dma_start(
                 out=ws_raw[32 * q : 32 * q + 4, :, :].bitcast(I32),
                 in_=w_scales[:, 4 * q : 4 * q + 4, :].rearrange("a r n -> r a n").bitcast(I32),
             )
-
-        def load_x(a, t):
+        for plane in range(1, PASSES * PACK):
+            a, t = divmod(plane, PACK)
+            if plane == PASSES * PACK - 1:
+                nc.sync.dma_start(out=w_raw[0][:].bitcast(I32), in_=wv[0])
             nc.sync.dma_start(out=x_pl[a][t][:], in_=xv[a, t])
-
-        nc.vector.memset(ws_raw[:].rearrange("p a n -> p (a n)").bitcast(I32), 0)
-
-        nc.sync.dma_start(out=tb_pl[0][:], in_=tbv[0])
-        nc.sync.dma_start(l3[:], offs3)
-        nc.sync.dma_start(out=tb_pl[1][:], in_=tbv[1])
-        nc.sync.dma_start(l2[:], offs2)
-        nc.sync.dma_start(out=tb_pl[2][:], in_=tbv[2])
-        nc.sync.dma_start(l1[:], offs)
-        load_x(0, 0)
-        nc.sync.dma_start(out=fk_sb[:], in_=fk.rearrange("(a p t) o -> p a (t o)", a=PASSES, t=PACK))
-        load_x(0, 1)
-        load_scales(0)
-        load_w(0)
-        load_scales(1)
-        load_x(0, 2)
-        load_scales(2)
-        load_x(0, 3)
-        load_scales(3)
-        load_w(1)
-        for t in range(PACK):
-            load_x(1, t)
-        nc.sync.dma_start(out=tb_pl[3][:], in_=tbv[3])
         nc.sync.dma_start(out=wb_raw[:], in_=wb.rearrange("(p t) n -> p t n", t=PACK))
         nc.sync.dma_start(l4[:], offs4)
         for h in range(2):
@@ -93,18 +86,14 @@ def tile_list_steps_tworeach_timeslook_kernel(tc, xf, fk, w_words, w_scales, tb,
 
         d = keep.tile([P, PACK, J], F32, name="d")
         t3 = keep.tile([P, PACK, J], F32, name="t3")
-        t2 = keep.tile([P, J], F32, name="t2")
-
-        def table_difference(t):
-            nc.scalar.activation(t3[:, t, :], tb_pl[t][:].indirect(l3[:]), ACT.Copy)
-            if t < PACK - 1:
-                nc.vector.tensor_tensor(d[:, t, :], tb_pl[t][:].indirect(l2[:]), t3[:, t, :], ALU.subtract)
-            else:
-                nc.scalar.activation(t2[:], tb_pl[t][:].indirect(l2[:]), ACT.Copy)
-                nc.vector.tensor_tensor(d[:, t, :], t2[:], t3[:, t, :], ALU.subtract)
-
-        for t in range(PACK - 1):
-            table_difference(t)
+        t2 = keep.tile([P, 2, J], F32, name="t2")
+        for t in range(2):
+            nc.scalar.activation(t3[:, t, :], tb_lo[t][:].indirect(l3[:]), ACT.Copy)
+            nc.vector.tensor_tensor(d[:, t, :], tb_lo[t][:].indirect(l2[:]), t3[:, t, :], ALU.subtract)
+        for t in range(2):
+            nc.scalar.activation(t3[:, 2 + t, :], tb_hi[:, t, :].indirect(l3[:]), ACT.Copy)
+            nc.scalar.activation(t2[:, t, :], tb_hi[:, t, :].indirect(l2[:]), ACT.Copy)
+        nc.vector.tensor_tensor(d[:, 2:4, :], t2[:], t3[:, 2:4, :], ALU.subtract)
 
         w_c = [keep.tile([P, R], U32, name=f"wc{a}", align_bytes=64) for a in range(PASSES)]
         w_s = keep.tile([P, PASSES, R], U8, name="ws", align_bytes=64)
@@ -113,66 +102,82 @@ def tile_list_steps_tworeach_timeslook_kernel(tc, xf, fk, w_words, w_scales, tb,
                 out=w_c[a][:].rearrange("p (t c i) -> p c t i", t=PACK, i=4),
                 in_=w_raw[a][:].rearrange("p (c i t) -> p c t i", t=PACK, i=4),
             )
-        for a in range(PASSES):
-            nc.vector.tensor_copy(
-                out=w_s[:, a, :].rearrange("p (t m) -> p t m", t=PACK),
-                in_=ws_raw[:, a, :].rearrange("p (m t) -> p t m", t=PACK),
-            )
+        nc.vector.tensor_copy(
+            out=w_s[:].rearrange("p a (t m) -> p a t m", t=PACK),
+            in_=ws_raw[:].rearrange("p a (m t) -> p a t m", t=PACK),
+        )
 
-        acc = [psum.tile([P, PACK, HALF], F32, name=f"acc{b}") for b in range(2)]
+        acc = [[psum.tile([P, 2, HALF], F32, name=f"acc{b}{c}") for c in range(2)] for b in range(2)]
         for a in range(PASSES):
-            g = keep.tile([P, PACK, LEAD + J], F32, name=f"g{a}")
-            nc.vector.memset(g[:, :, 0:LEAD], 0.0)
+            g = gs[a]
             e = keep.tile([P, PACK, J], F32, name=f"e{a}")
-            ub = keep.tile([P, PACK, J], BF16, name=f"ub{a}")
             uw = keep.tile([P, J * PACK], BF16, name=f"uw{a}", align_bytes=64)
             u_c = keep.tile([P, J], U32, name=f"uc{a}", align_bytes=64)
             u_s = keep.tile([P, J], U8, name=f"us{a}", align_bytes=64)
+            if a == 0:
+                ub = keep.tile([P, PACK, J], BF16, name="ub")
+                uv = ub[:]
+            else:
+                uv = uw[:].rearrange("p (j t) -> p t j", t=PACK)
             for t in range(PACK):
-                nc.scalar.activation(g[:, t, LEAD:], x_pl[a][t][:].indirect(l1[:]), ACT.Copy)
-                nc.vector.scalar_tensor_tensor(
-                    out=e[:, t, :], in0=g[:, t, LEAD - 1 : LEAD - 1 + J], scalar=-0.6, in1=g[:, t, LEAD:], op0=ALU.mult, op1=ALU.add
-                )
-                nc.vector.tensor_scalar_mul(ub[:, t, :], e[:, t, :], fk_sb[:, a, t : t + 1])
+                cuts = [(0, HALF), (HALF, J)] if (a, t) == (PASSES - 1, PACK - 1) else [(0, J)]
+                if (a, t) == (PASSES - 1, PACK - 1):
+                    nc.scalar.activation(g[:, t, LEAD : LEAD + HALF], x_pl[a][t][:].indirect(l1[:, 0 : HALF // 16]), ACT.Copy)
+                    nc.vector.tensor_copy(g[:, t, LEAD + HALF :], x_pl[a][t][:].indirect(l1[:, HALF // 16 :]))
+                else:
+                    nc.scalar.activation(g[:, t, LEAD:], x_pl[a][t][:].indirect(l1[:]), ACT.Copy)
+                for j0, j1 in cuts:
+                    nc.vector.scalar_tensor_tensor(
+                        out=e[:, t, j0:j1],
+                        in0=g[:, t, LEAD - 1 + j0 : LEAD - 1 + j1],
+                        scalar=-0.6,
+                        in1=g[:, t, LEAD + j0 : LEAD + j1],
+                        op0=ALU.mult,
+                        op1=ALU.add,
+                    )
+                for j0, j1 in cuts:
+                    nc.vector.tensor_scalar_mul(uv[:, t, j0:j1], e[:, t, j0:j1], fk_sb[:, a, t : t + 1])
+            if a == 0:
+                nc.vector.tensor_copy(out=weave_out(uw[:]), in_=weave_in(ub[:]))
+                nc.vector.quantize_mx(out=u_c[:].bitcast(E4M3), scales=u_s[:], in_=uw[:])
             for b in range(2):
                 js = slice(b * HALF, (b + 1) * HALF)
-                nc.vector.tensor_copy(out=weave_out(uw[:, b * HALF * PACK : (b + 1) * HALF * PACK]), in_=weave_in(ub[:, :, js]))
-            for b in range(2):
-                js = slice(b * HALF, (b + 1) * HALF)
-                nc.vector.quantize_mx(out=u_c[:, js].bitcast(E4M3), scales=u_s[:, js], in_=uw[:, b * HALF * PACK : (b + 1) * HALF * PACK])
+                if a == 1:
+                    nc.vector.quantize_mx(out=u_c[:, js].bitcast(E4M3), scales=u_s[:, js], in_=uw[:, b * HALF * PACK : (b + 1) * HALF * PACK])
                 for t in range(PACK):
                     ms = slice(t * P, (t + 1) * P)
                     nc.tensor.matmul_mx(
-                        out=acc[b][:, t, :],
+                        out=acc[b][t // 2][:, t % 2, :],
                         lhsT=w_c[a][:, ms].bitcast(E5M2),
                         lhsT_scale=w_s[:, a, ms],
                         rhs=u_c[:, js].bitcast(E4M3),
                         rhs_scale=u_s[:, js],
-                        start=(a == 0 and t == 0),
-                        stop=(a == PASSES - 1 and t == PACK - 1),
+                        start=(a == 0 and t % 2 == 0),
+                        stop=(a == PASSES - 1 and t % 2 == 1),
                     )
-
-        table_difference(PACK - 1)
 
         wbw = keep.tile([P, N * PACK], BF16, name="wbw", align_bytes=64)
         wb_c = keep.tile([P, N], U32, name="wbc", align_bytes=64)
         wb_s = keep.tile([P, N], U8, name="wbs", align_bytes=64)
         nc.scalar.copy(out=weave_out(wbw[:]), in_=weave_in(wb_raw[:]))
-        nc.vector.quantize_mx(out=wb_c[:].bitcast(E5M2), scales=wb_s[:], in_=wbw[:])
 
-        s = [keep.tile([P, PACK, HALF], F32, name=f"s{b}") for b in range(2)]
+        shared = keep.tile([P, 3 * J], F32, name="shared")
+        s1 = keep.tile([P, PACK, HALF], F32, name="s1")
+        s = [shared[:, J:].rearrange("p (t j) -> p t j", t=PACK), s1[:]]
+        tzg = shared[:, 0 : 2 * J].rearrange("p (h j) -> p h j", h=2)
         hw = [keep.tile([P, HALF * PACK], BF16, name=f"hw{b}", align_bytes=64) for b in range(2)]
         h_c = [keep.tile([P, HALF], U32, name=f"hc{b}", align_bytes=64) for b in range(2)]
         h_s = [keep.tile([P, HALF], U8, name=f"hs{b}", align_bytes=64) for b in range(2)]
         pr = [psum.tile([P, 2, HALF], F32, name=f"pr{b}") for b in range(2)]
         res = [keep.tile([P, 2, HALF], F32, name=f"res{b}") for b in range(2)]
-        tzg = keep.tile([P, 2, J], F32, name="tzg")
+        nc.scalar.activation(tzg[:, 0, :], tz_sb[0][:].indirect(l4[:]), ACT.Copy)
         for b in range(2):
-            nc.vector.tensor_tensor(s[b][:], acc[b][:], d[:, :, b * HALF : (b + 1) * HALF], ALU.add)
-        nc.scalar.activation(weave_out(hw[0][:]), weave_in(s[0][:]), ACT.Relu)
-        nc.vector.tensor_scalar_max(weave_out(hw[1][:]), weave_in(s[1][:]), 0.0)
-        for h in range(2):
-            nc.scalar.activation(tzg[:, h, :], tz_sb[h][:].indirect(l4[:]), ACT.Copy)
+            for c in range(2):
+                nc.vector.tensor_tensor(s[b][:, 2 * c : 2 * c + 2, :], acc[b][c][:], d[:, 2 * c : 2 * c + 2, b * HALF : (b + 1) * HALF], ALU.add)
+        nc.vector.quantize_mx(out=wb_c[:].bitcast(E5M2), scales=wb_s[:], in_=wbw[:])
+        nc.scalar.activation(weave_out(hw[0][:]), weave_in(s[0]), ACT.Relu)
+        nc.vector.tensor_scalar_max(weave_out(hw[1][:]), weave_in(s[1]), 0.0)
+        nc.scalar.activation(tzg[:, 1, :], tz_sb[1][:].indirect(l4[:]), ACT.Copy)
         for b in range(2):
             nc.vector.quantize_mx(out=h_c[b][:].bitcast(E5M2), scales=h_s[b][:], in_=hw[b][:])
             for h in range(2):
@@ -186,6 +191,7 @@ def tile_list_steps_tworeach_timeslook_kernel(tc, xf, fk, w_words, w_scales, tb,
                     start=True,
                     stop=True,
                 )
+
         ov = out.rearrange("(h p) j -> p h j", p=P)
         for b in range(2):
             js = slice(b * HALF, (b + 1) * HALF)

from contextlib import ExitStack

import concourse.mybir as mybir

K, T, J, R, V, N, Z = 1024, 1024, 256, 512, 512, 256, 512
FLOPS = 2 * K * R * J + 2 * R * N * J

F32 = mybir.dt.float32
BF16 = mybir.dt.bfloat16
I32 = mybir.dt.int32
U32 = mybir.dt.uint32
U16 = mybir.dt.uint16
U8 = mybir.dt.uint8
E4M3 = mybir.dt.float8_e4m3fn_x4
E5M2 = mybir.dt.float8_e5m2_x4
ALU = mybir.AluOpType
ACT = mybir.ActivationFunctionType

P = 128
PACK = 4
PASSES = K // (P * PACK)
HALF = J // 2
LEAD = 8


def weave_out(tile_ap):
    return tile_ap.rearrange("p (c i t) -> p c t i", i=4, t=PACK)


def weave_in(planes_ap):
    return planes_ap.rearrange("p t (c i) -> p c t i", i=4)


def tile_list_steps_tworeach_timeslook_kernel(tc, xf, fk, w_words, w_scales, tb, wb, tz, offs, offs2, offs3, offs4, out):
    nc = tc.nc
    with ExitStack() as ctx:
        keep = ctx.enter_context(tc.tile_pool(name="keep", bufs=1))
        psum = ctx.enter_context(tc.psum_pool(name="psum", bufs=1))

        l1 = keep.tile([P, J // 16], U16, name="l1")
        l2 = keep.tile([P, J // 16], U16, name="l2")
        l3 = keep.tile([P, J // 16], U16, name="l3")
        l4 = keep.tile([P, J // 16], U16, name="l4")
        x_pl = [[keep.tile([P, T], F32, name=f"x{a}{t}") for t in range(PACK)] for a in range(PASSES)]
        tb_lo = [keep.tile([P, V], F32, name=f"tb{t}") for t in range(2)]
        tb_hi = keep.tile([P, 2, V], F32, name="tbhi")
        w_raw = [keep.tile([P, R], U32, name=f"wraw{a}") for a in range(PASSES)]
        ws_raw = keep.tile([P, PASSES, R], U8, name="wsraw")
        fk_sb = keep.tile([P, PASSES, 8], F32, name="fk")
        wb_raw = keep.tile([P, PACK, N], F32, name="wbraw")
        tz_sb = [keep.tile([P, Z], F32, name=f"tz{h}") for h in range(2)]

        xv = xf.rearrange("(a p t) c -> a t p c", a=PASSES, t=PACK)
        tbv = tb.rearrange("(p t) v -> p t v", t=PACK)

        wv = w_words.rearrange("a p n t -> a p (n t)").bitcast(I32)

        gs = [keep.tile([P, PACK, LEAD + J], F32, name=f"g{a}") for a in range(PASSES)]
        nc.vector.memset(gs[0][:, :, 0:LEAD], 0.0)
        nc.scalar.activation(gs[1][:, :, 0:LEAD], gs[0][:, :, 0:LEAD], ACT.Copy)
        nc.gpsimd.memset(ws_raw[:].rearrange("p a n -> p (a n)").bitcast(I32), 0)

        nc.sync.dma_start(out=tb_lo[0][:], in_=tbv[:, 0, :])
        nc.sync.dma_start(l3[:], offs3)
        nc.sync.dma_start(l2[:], offs2)
        nc.sync.dma_start(out=tb_lo[1][:], in_=tbv[:, 1, :])
        nc.sync.dma_start(out=tb_hi[:], in_=tbv[:, 2:4, :])
        nc.sync.dma_start(l1[:], offs)
        nc.sync.dma_start(out=w_raw[1][:].bitcast(I32), in_=wv[1])
        nc.sync.dma_start(out=x_pl[0][0][:], in_=xv[0, 0])
        nc.sync.dma_start(out=fk_sb[:, :, 0:PACK], in_=fk.rearrange("(a p t) o -> p a (t o)", a=PASSES, t=PACK))
        for q in range(4):
            nc.sync.dma_start(
                out=ws_raw[32 * q : 32 * q + 4, :, :].bitcast(I32),
                in_=w_scales[:, 4 * q : 4 * q + 4, :].rearrange("a r n -> r a n").bitcast(I32),
            )
        for plane in range(1, PASSES * PACK):
            a, t = divmod(plane, PACK)
            if plane == PASSES * PACK - 1:
                nc.sync.dma_start(out=w_raw[0][:].bitcast(I32), in_=wv[0])
            nc.sync.dma_start(out=x_pl[a][t][:], in_=xv[a, t])
        nc.sync.dma_start(out=wb_raw[:], in_=wb.rearrange("(p t) n -> p t n", t=PACK))
        nc.sync.dma_start(l4[:], offs4)
        for h in range(2):
            nc.sync.dma_start(out=tz_sb[h][:], in_=tz[h * P : (h + 1) * P, :])

        d = keep.tile([P, PACK, J], F32, name="d")
        t3 = keep.tile([P, PACK, J], F32, name="t3")
        t2 = keep.tile([P, 2, J], F32, name="t2")
        for t in range(2):
            nc.scalar.activation(t3[:, t, :], tb_lo[t][:].indirect(l3[:]), ACT.Copy)
            nc.vector.tensor_tensor(d[:, t, :], tb_lo[t][:].indirect(l2[:]), t3[:, t, :], ALU.subtract)
        for t in range(2):
            nc.scalar.activation(t3[:, 2 + t, :], tb_hi[:, t, :].indirect(l3[:]), ACT.Copy)
            nc.scalar.activation(t2[:, t, :], tb_hi[:, t, :].indirect(l2[:]), ACT.Copy)
        nc.vector.tensor_tensor(d[:, 2:4, :], t2[:], t3[:, 2:4, :], ALU.subtract)

        w_c = [keep.tile([P, R], U32, name=f"wc{a}", align_bytes=64) for a in range(PASSES)]
        w_s = keep.tile([P, PASSES, R], U8, name="ws", align_bytes=64)
        for a in range(PASSES):
            nc.vector.tensor_copy(
                out=w_c[a][:].rearrange("p (t c i) -> p c t i", t=PACK, i=4),
                in_=w_raw[a][:].rearrange("p (c i t) -> p c t i", t=PACK, i=4),
            )
        nc.vector.tensor_copy(
            out=w_s[:].rearrange("p a (t m) -> p a t m", t=PACK),
            in_=ws_raw[:].rearrange("p a (m t) -> p a t m", t=PACK),
        )

        acc = [[psum.tile([P, 2, HALF], F32, name=f"acc{b}{c}") for c in range(2)] for b in range(2)]
        for a in range(PASSES):
            g = gs[a]
            e = keep.tile([P, PACK, J], F32, name=f"e{a}")
            uw = keep.tile([P, J * PACK], BF16, name=f"uw{a}", align_bytes=64)
            u_c = keep.tile([P, J], U32, name=f"uc{a}", align_bytes=64)
            u_s = keep.tile([P, J], U8, name=f"us{a}", align_bytes=64)
            if a == 0:
                ub = keep.tile([P, PACK, J], BF16, name="ub")
                uv = ub[:]
            else:
                uv = uw[:].rearrange("p (j t) -> p t j", t=PACK)
            for t in range(PACK):
                cuts = [(0, HALF), (HALF, J)] if (a, t) == (PASSES - 1, PACK - 1) else [(0, J)]
                if (a, t) == (PASSES - 1, PACK - 1):
                    nc.scalar.activation(g[:, t, LEAD : LEAD + HALF], x_pl[a][t][:].indirect(l1[:, 0 : HALF // 16]), ACT.Copy)
                    nc.vector.tensor_copy(g[:, t, LEAD + HALF :], x_pl[a][t][:].indirect(l1[:, HALF // 16 :]))
                else:
                    nc.scalar.activation(g[:, t, LEAD:], x_pl[a][t][:].indirect(l1[:]), ACT.Copy)
                for j0, j1 in cuts:
                    nc.vector.scalar_tensor_tensor(
                        out=e[:, t, j0:j1],
                        in0=g[:, t, LEAD - 1 + j0 : LEAD - 1 + j1],
                        scalar=-0.6,
                        in1=g[:, t, LEAD + j0 : LEAD + j1],
                        op0=ALU.mult,
                        op1=ALU.add,
                    )
                for j0, j1 in cuts:
                    nc.vector.tensor_scalar_mul(uv[:, t, j0:j1], e[:, t, j0:j1], fk_sb[:, a, t : t + 1])
            if a == 0:
                nc.vector.tensor_copy(out=weave_out(uw[:]), in_=weave_in(ub[:]))
                nc.vector.quantize_mx(out=u_c[:].bitcast(E4M3), scales=u_s[:], in_=uw[:])
            for b in range(2):
                js = slice(b * HALF, (b + 1) * HALF)
                if a == 1:
                    nc.vector.quantize_mx(out=u_c[:, js].bitcast(E4M3), scales=u_s[:, js], in_=uw[:, b * HALF * PACK : (b + 1) * HALF * PACK])
                for t in range(PACK):
                    ms = slice(t * P, (t + 1) * P)
                    nc.tensor.matmul_mx(
                        out=acc[b][t // 2][:, t % 2, :],
                        lhsT=w_c[a][:, ms].bitcast(E5M2),
                        lhsT_scale=w_s[:, a, ms],
                        rhs=u_c[:, js].bitcast(E4M3),
                        rhs_scale=u_s[:, js],
                        start=(a == 0 and t % 2 == 0),
                        stop=(a == PASSES - 1 and t % 2 == 1),
                    )

        wbw = keep.tile([P, N * PACK], BF16, name="wbw", align_bytes=64)
        wb_c = keep.tile([P, N], U32, name="wbc", align_bytes=64)
        wb_s = keep.tile([P, N], U8, name="wbs", align_bytes=64)
        nc.scalar.copy(out=weave_out(wbw[:]), in_=weave_in(wb_raw[:]))

        shared = keep.tile([P, 3 * J], F32, name="shared")
        s1 = keep.tile([P, PACK, HALF], F32, name="s1")
        s = [shared[:, J:].rearrange("p (t j) -> p t j", t=PACK), s1[:]]
        tzg = shared[:, 0 : 2 * J].rearrange("p (h j) -> p h j", h=2)
        hw = [keep.tile([P, HALF * PACK], BF16, name=f"hw{b}", align_bytes=64) for b in range(2)]
        h_c = [keep.tile([P, HALF], U32, name=f"hc{b}", align_bytes=64) for b in range(2)]
        h_s = [keep.tile([P, HALF], U8, name=f"hs{b}", align_bytes=64) for b in range(2)]
        pr = [psum.tile([P, 2, HALF], F32, name=f"pr{b}") for b in range(2)]
        res = [keep.tile([P, 2, HALF], F32, name=f"res{b}") for b in range(2)]
        nc.scalar.activation(tzg[:, 0, :], tz_sb[0][:].indirect(l4[:]), ACT.Copy)
        for b in range(2):
            for c in range(2):
                nc.vector.tensor_tensor(s[b][:, 2 * c : 2 * c + 2, :], acc[b][c][:], d[:, 2 * c : 2 * c + 2, b * HALF : (b + 1) * HALF], ALU.add)
        nc.vector.quantize_mx(out=wb_c[:].bitcast(E5M2), scales=wb_s[:], in_=wbw[:])
        nc.scalar.activation(weave_out(hw[0][:]), weave_in(s[0]), ACT.Relu)
        nc.vector.tensor_scalar_max(weave_out(hw[1][:]), weave_in(s[1]), 0.0)
        nc.scalar.activation(tzg[:, 1, :], tz_sb[1][:].indirect(l4[:]), ACT.Copy)
        for b in range(2):
            nc.vector.quantize_mx(out=h_c[b][:].bitcast(E5M2), scales=h_s[b][:], in_=hw[b][:])
            for h in range(2):
                ns = slice(h * P, (h + 1) * P)
                nc.tensor.matmul_mx(
                    out=pr[b][:, h, :],
                    lhsT=wb_c[:, ns].bitcast(E5M2),
                    lhsT_scale=wb_s[:, ns],
                    rhs=h_c[b][:].bitcast(E5M2),
                    rhs_scale=h_s[b][:],
                    start=True,
                    stop=True,
                )

        ov = out.rearrange("(h p) j -> p h j", p=P)
        for b in range(2):
            js = slice(b * HALF, (b + 1) * HALF)
            nc.vector.tensor_tensor(res[b][:], pr[b][:], tzg[:, :, js], ALU.mult)
            nc.sync.dma_start(out=ov[:, :, js], in_=res[b][:])
